import numpy as np, ml_dtypes
CORES = [10,14,66,70,74,78,82,86,90,94,106,110]
N = 12
import mx_ref
NC, G = 128, 4
EPS = 0.001
BF = ml_dtypes.bfloat16
def cut(t, i, w=512):
    return t[:, w * i:w * i + w]
def tile(rs):
    return np.stack(rs, axis=2).reshape(128, -1).astype(BF)
def layer(w, X):
    out = []
    for i in range(G):
        for t in range(len(X)):
            p = mx_ref.matmul(mx_ref.quantize(cut(w, len(X) * i + t)), X[t])
            z = p if t == 0 else z + p
        out.append(z)
    return out
def normed(Z, s):
    return [z * f for z, f in zip(Z, s)]
def setup_inputs(rng):
    def f(*shape):
        return mx_ref.flush((rng.standard_normal(shape, dtype=np.float32) * np.exp2(rng.integers(-2, 3, shape[:-1] + (1,)))).astype(BF))
    return {"x": f(N, 128, 4 * NC), "w1": f(N, 128, G * 512), "w2": f(N, 128, 512)}
def setup_inputs_blocks(rng):
    d = setup_inputs(rng)
    for k in ("x", "w1", "w2"): d[k] = mx_ref.spread(d[k], rng, 4)
    return d
def setup_inputs_wide(rng):
    d = setup_inputs(rng)
    for k in ("x", "w1", "w2"): d[k] = mx_ref.flush((d[k].astype(np.float32) * np.exp2(rng.integers(-5, 6, (N, 1, 1))).astype(np.float32)).astype(BF))
    return d
def setup_inputs_rows(rng):
    d = setup_inputs(rng); v = d["w1"].astype(np.float32).reshape(N, 128, -1, 4)
    d["w1"] = mx_ref.flush((v * np.exp2(rng.integers(-6, 7, (N, 1, v.shape[2], 1))).astype(np.float32)).reshape(d["w1"].shape).astype(BF))
    return d
def setup_inputs_faint(rng):
    d = setup_inputs(rng); d["x"] = mx_ref.flush((d["x"].astype(np.float32) * np.float32(2.0 ** -12)).astype(BF))
    return d
def reference(x, w1, w2, own=None):
    Z = [layer(w1[r], [mx_ref.quantize(x[r])]) for r in range(N)]
    ms = [sum((Z[r][i].astype(np.float64) ** 2).sum(axis=1, keepdims=True) for r in range(N)) / (N * NC) for i in range(G)]
    s = [(1 / np.sqrt(m + EPS)).astype(np.float32) for m in ms]
    h = np.stack([tile(normed(Z[r], s)) for r in range(N)])
    use = h if own is None else own["h"]
    H = [mx_ref.quantize(use[j]) for j in range(N)]
    y = np.zeros((N, 128, N * NC), np.float32)
    for r in range(N):
        qw = mx_ref.quantize(w2[r])
        for j in range(N):
            y[r][:, NC * j:NC * j + NC] = mx_ref.matmul(qw, H[j])
    return {"h": h, "y": y}

@@ -1,0 +1,240 @@
+from concourse.bass import DstId, RemoteDMATransfer
+from concourse.mybir import dt, AluOpType, AxisListType, ActivationFunctionType
+
+N = 12
+NC = 128
+EPS = 0.001
+NCH = 6
+WAVE_A = (1, 2, 3)
+WAVE_B = (4, 5)
+
+SCRATCH = {
+    "xb": ("sbuf", [128, 512], "bfloat16"),
+    "w1b": ("sbuf", [128, 2048], "bfloat16"),
+    "w2b": ("sbuf", [128, 512], "bfloat16"),
+    "xq": ("sbuf", [128, 128], "float8_e4m3fn_x4"),
+    "xs": ("sbuf", [128, 128], "uint8"),
+    "w1q": ("sbuf", [128, 512], "float8_e4m3fn_x4"),
+    "w1s": ("sbuf", [128, 512], "uint8"),
+    "w2q": ("sbuf", [128, 128], "float8_e4m3fn_x4"),
+    "w2s": ("sbuf", [128, 128], "uint8"),
+    "z": ("psum", [128, 2048], "float32"),
+    "yp": ("psum", [128, 2048], "float32"),
+    "junk": ("sbuf", [128, 512], "float32"),
+    "junk2": ("sbuf", [128, 16], "float32"),
+    "ssl": ("sbuf", [128, 4 * NCH], "float32"),
+    "part": ("sbuf", [128, 4], "float32"),
+    "oth": ("sbuf", [128, 4], "float32"),
+    "tot": ("sbuf", [128, 4], "float32"),
+    "rt": ("sbuf", [128, 4], "float32"),
+    "sc": ("sbuf", [128, 4], "float32"),
+    "hb": ("sbuf", [128, 512], "bfloat16"),
+    "hq": ("sbuf", [128, N * 128], "float8_e4m3fn_x4"),
+    "hs": ("sbuf", [128, N * 128], "uint8"),
+    "yb": ("sbuf", [128, N * 128], "float32"),
+}
+SEMAPHORES = ["ldx", "ldwa", "ldwb", "ldw2", "qx", "qa", "qb", "qw2", "mm0", "mm1", "mm2", "mm3", "sq", "ssarr", "pr",
+              "ss2", "tt", "rtd", "sd", "hd", "hqd", "tA", "tB", "tP", "fA", "fB", "mA", "mB", "mC", "mD1", "mD2",
+              "cpA", "cpB", "cpC", "cpD", "fBl", "lsem", "st"]
+
+
+def _bits(m):
+    return bin(m).count("1")
+
+
+def _runs(blocks):
+    out = []
+    for b in sorted(blocks):
+        if out and out[-1][1] == b:
+            out[-1][1] = b + 1
+        else:
+            out.append([b, b + 1])
+    return out
+
+
+def rank_program(g, core, T, topo):
+    rank = T.rank_of(core)
+    if rank is None:
+        return
+    S = T.sem
+    A = ActivationFunctionType
+    chips = []
+    for c in T.cores:
+        if topo.chip(c) not in chips:
+            chips.append(topo.chip(c))
+    at = {}
+    for c in T.cores:
+        at[(chips.index(topo.chip(c)), topo.die(c))] = c
+    q, d = chips.index(topo.chip(core)), topo.die(core)
+    partner = [c for c in T.cores if topo.chip(c) == topo.chip(core) and c != core][0]
+    od = topo.die(partner)
+
+    def peer(k):
+        return at[((q + k) % NCH, d)]
+
+    def dst(c):
+        rid, pid, _ = topo.addr(c)
+        return DstId(rid=rid, pnc=pid)
+
+    on = topo.mask(core, partner)
+    off = on
+    for k in range(1, NCH):
+        off &= topo.mask(core, peer(k))
+    hi = on & ~off
+    n_on, n_off, n_hi = _bits(on), _bits(off), _bits(hi)
+    lcount = [0]
+
+    def codes(a, b):
+        return T.hq[:, 128 * a:128 * b].bitcast(dt.uint8)
+
+    def plane(a, b):
+        return T.hs[:, 128 * a:128 * b]
+
+    def block_of(slot):
+        k, dd = (slot, d) if slot < NCH else (slot - NCH, od)
+        return T.rank_of(at[((q - k) % NCH, dd)])
+
+    g.sync.dma_start(T.xb[:], T.x[:, :]).then_inc(S.ldx, 16)
+    g.scalar.dma_start(T.w1b[:, 0:1024], T.w1[:, 0:1024]).then_inc(S.ldwa, 16)
+    g.sync.dma_start(T.w1b[:, 1024:2048], T.w1[:, 1024:2048]).then_inc(S.ldwb, 16)
+    g.scalar.dma_start(T.w2b[:], T.w2[:, :]).then_inc(S.ldw2, 16)
+
+    v = g.vector
+    v.wait_ge(S.ldx, 16)
+    v.quantize_mx(T.xq[:], T.xs[:], T.xb[:]).then_inc(S.qx, 1)
+    v.wait_ge(S.ldwa, 16)
+    v.quantize_mx(T.w1q[:, 0:256], T.w1s[:, 0:256], T.w1b[:, 0:1024]).then_inc(S.qa, 1)
+    v.wait_ge(S.ldwb, 16)
+    v.quantize_mx(T.w1q[:, 256:512], T.w1s[:, 256:512], T.w1b[:, 1024:2048]).then_inc(S.qb, 1)
+    v.wait_ge(S.ldw2, 16)
+    v.quantize_mx(T.w2q[:], T.w2s[:], T.w2b[:]).then_inc(S.qw2, 1)
+
+    te = g.tensor
+    te.wait_ge(S.qx, 1)
+    te.wait_ge(S.qa, 1)
+    for i in range(4):
+        if i == 2:
+            te.wait_ge(S.qb, 1)
+        te.matmul_mx(T.z[:, 512 * i:512 * i + 128], T.w1q[:, 128 * i:128 * i + 128], T.w1s[:, 128 * i:128 * i + 128],
+                     T.xq[:], T.xs[:], True, True).then_inc(S["mm%d" % i], 1)
+    sc = g.scalar
+    for i in range(4):
+        sc.wait_ge(S["mm%d" % i], 1)
+        sc.activation(T.junk[:, 128 * i:128 * i + 128], T.z[:, 512 * i:512 * i + 128], A.Square,
+                      accum_out=T.ssl[:, i:i + 1]).then_inc(S.sq, 1)
+
+    g.wait_ge(S.sq, 4)
+    g.remote_dma_fused([RemoteDMATransfer(dst_ids=[dst(peer(k)) for k in range(1, NCH)], dma_engine_mask=off,
+                                          remote_sem=S.ssarr, srcs=[T.ssl[:, 0:4]],
+                                          dsts=[T.ssl[:, 4 * k:4 * k + 4] for k in range(1, NCH)])], local_sem=S.lsem)
+    lcount[0] += n_off
+    arr = n_off * (NCH - 1)
+    v.wait_ge(S.sq, 4)
+    v.wait_ge(S.ssarr, arr)
+    for i in (0, 1):
+        v.tensor_reduce(T.part[:, i:i + 1], T.ssl[:, i:4 * NCH:4], AxisListType.X, AluOpType.add).then_inc(S.pr, 1)
+    sc.wait_ge(S.sq, 4)
+    sc.wait_ge(S.ssarr, arr)
+    for i in (2, 3):
+        sc.activation(T.junk2[:, 8 * (i - 2):8 * (i - 2) + NCH], T.ssl[:, i:4 * NCH:4], A.Identity,
+                      accum_out=T.part[:, i:i + 1]).then_inc(S.pr, 1)
+    rid, pid, _ = topo.addr(partner)
+    g.wait_ge(S.pr, 4)
+    g.remote_dma(T.oth[:], T.part[:], S.ss2, S.lsem, pid, rid, off)
+    lcount[0] += n_off
+    v.wait_ge(S.pr, 4)
+    v.wait_ge(S.ss2, n_off)
+    v.tensor_tensor(T.tot[:], T.part[:], T.oth[:], AluOpType.add).then_inc(S.tt, 1)
+    sc.wait_ge(S.tt, 1)
+    sc.activation(T.rt[:], T.tot[:], A.Sqrt, bias=EPS, scale=1.0 / (N * NC)).then_inc(S.rtd, 1)
+    v.wait_ge(S.rtd, 1)
+    v.reciprocal(T.sc[:], T.rt[:]).then_inc(S.sd, 1)
+
+    v.wait_ge(S.sd, 1)
+    for b in (0, 1):
+        v.tensor_scalar(T.hb[:, b:512:4], T.z[:, 512 * b:512 * b + 128], T.sc[:, b:b + 1], None,
+                        AluOpType.mult).then_inc(S.hd, 1)
+    sc.wait_ge(S.sd, 1)
+    for b in (2, 3):
+        sc.activation(T.hb[:, b:512:4], T.z[:, 512 * b:512 * b + 128], A.Identity,
+                      scale=T.sc[:, b:b + 1]).then_inc(S.hd, 1)
+    v.wait_ge(S.hd, 4)
+    v.quantize_mx(T.hq[:, 0:128], T.hs[:, 0:128], T.hb[:]).then_inc(S.hqd, 1)
+
+    g.wait_ge(S.hqd, 1)
+    for wave, sem in ((WAVE_A, S.tA), (WAVE_B, S.tB)):
+        ids = [dst(peer(k)) for k in wave]
+        g.remote_dma_fused([RemoteDMATransfer(dst_ids=ids, dma_engine_mask=off, remote_sem=sem, srcs=[plane(0, 1)],
+                                              dsts=[plane(k, k + 1) for k in wave])], local_sem=S.lsem)
+        g.remote_dma_fused([RemoteDMATransfer(dst_ids=ids, dma_engine_mask=off, remote_sem=sem, srcs=[codes(0, 1)],
+                                              dsts=[codes(k, k + 1) for k in wave])], local_sem=S.lsem)
+        lcount[0] += 2 * n_off
+    g.remote_dma(plane(NCH, NCH + 1), plane(0, 1), S.tP, S.lsem, pid, rid, hi)
+    g.remote_dma(codes(NCH, NCH + 1), codes(0, 1), S.tP, S.lsem, pid, rid, hi)
+    lcount[0] += 2 * n_hi
+    nA, nB = 2 * n_off * len(WAVE_A), 2 * n_off * len(WAVE_B)
+    a0, a1 = WAVE_A[0], WAVE_A[-1] + 1
+    b0, b1 = WAVE_B[0], WAVE_B[-1] + 1
+    g.wait_ge(S.tA, nA)
+    g.remote_dma(plane(NCH + a0, NCH + a1), plane(a0, a1), S.fA, S.lsem, pid, rid, hi)
+    g.remote_dma(codes(NCH + a0, NCH + a1), codes(a0, a1), S.fA, S.lsem, pid, rid, hi)
+    lcount[0] += 2 * n_hi
+    g.wait_ge(S.tB, nB)
+    g.remote_dma(plane(NCH + b0, NCH + b1), plane(b0, b1), S.fB, S.fBl, pid, rid, on)
+    g.remote_dma(codes(NCH + b0, NCH + b1), codes(b0, b1), S.fB, S.fBl, pid, rid, on)
+    g.wait_ge(S.lsem, lcount[0])
+
+    def mm(out, a, b, sem):
+        te.matmul_mx(out, T.w2q[:], T.w2s[:], T.hq[:, 128 * a:128 * b], T.hs[:, 128 * a:128 * b],
+                     True, True).then_inc(sem, 1)
+
+    te.wait_ge(S.qw2, 1)
+    te.wait_ge(S.hqd, 1)
+    te.wait_ge(S.tA, nA)
+    mm(T.yp[:, 0:128 * a1], 0, a1, S.mA)
+    te.wait_ge(S.tB, nB)
+    mm(T.yp[:, 512:512 + 128 * (b1 - b0)], b0, b1, S.mB)
+    te.wait_ge(S.tP, 2 * n_hi)
+    te.wait_ge(S.fA, 2 * n_hi)
+    mm(T.yp[:, 1024:1024 + 128 * a1], NCH, NCH + a1, S.mC)
+    te.wait_ge(S.fB, 2 * n_on)
+    mm(T.yp[:, 1536:1536 + 128], NCH + b0, NCH + b0 + 1, S.mD1)
+    mm(T.z[:, 0:128], NCH + b0 + 1, NCH + b1, S.mD2)
+
+    def ycol(slot):
+        j = block_of(slot)
+        return T.yb[:, 128 * j:128 * j + 128]
+
+    v.wait_ge(S.mA, 1)
+    for t in range(a1):
+        v.tensor_copy(ycol(t), T.yp[:, 128 * t:128 * t + 128]).then_inc(S.cpA, 1)
+    v.wait_ge(S.mC, 1)
+    for t in range(a1):
+        v.tensor_copy(ycol(NCH + t), T.yp[:, 1024 + 128 * t:1024 + 128 * t + 128]).then_inc(S.cpC, 1)
+    v.wait_ge(S.mD1, 1)
+    v.tensor_copy(ycol(NCH + b0), T.yp[:, 1536:1536 + 128]).then_inc(S.cpD, 1)
+    sc.wait_ge(S.mB, 1)
+    for t in range(b1 - b0):
+        sc.activation(ycol(b0 + t), T.yp[:, 512 + 128 * t:512 + 128 * t + 128], A.Copy).then_inc(S.cpB, 1)
+    sc.wait_ge(S.mD2, 1)
+    sc.activation(ycol(NCH + b0 + 1), T.z[:, 0:128], A.Copy).then_inc(S.cpD, 1)
+
+    sy = g.sync
+    nst = 0
+    sy.wait_ge(S.hqd, 1)
+    sy.wait_ge(S.cpA, a1)
+    sy.wait_ge(S.cpC, a1)
+    sy.wait_ge(S.fBl, 2 * n_on)
+    early = [block_of(t) for t in range(a1)] + [block_of(NCH + t) for t in range(a1)]
+    for lo, hi_ in _runs(early):
+        sy.dma_start(T.y[:, 128 * lo:128 * hi_], T.yb[:, 128 * lo:128 * hi_]).then_inc(S.st, 16)
+        nst += 16
+    sy.dma_start(T.h[:, :], T.hb[:]).then_inc(S.st, 16)
+    nst += 16
+    sy.wait_ge(S.cpB, b1 - b0)
+    sy.wait_ge(S.cpD, 2)
+    late = [block_of(t) for t in range(b0, b1)] + [block_of(NCH + t) for t in range(b0, b1)]
+    for lo, hi_ in _runs(late):
+        sy.dma_start(T.y[:, 128 * lo:128 * hi_], T.yb[:, 128 * lo:128 * hi_]).then_inc(S.st, 16)
+        nst += 16
+    sy.wait_ge(S.st, nst)

@@ -23,8 +23,8 @@ SCRATCH = {
     "junk": ("sbuf", [128, 512], "float32"),
     "junk2": ("sbuf", [128, 16], "float32"),
     "ssl": ("sbuf", [128, 4 * NCH], "float32"),
-    "part": ("sbuf", [128, 4], "float32"),
-    "oth": ("sbuf", [128, 4], "float32"),
+    "own": ("sbuf", [128, 8], "float32"),
+    "oth": ("sbuf", [128, 8], "float32"),
     "tot": ("sbuf", [128, 4], "float32"),
     "rt": ("sbuf", [128, 4], "float32"),
     "sc": ("sbuf", [128, 4], "float32"),
@@ -33,9 +33,9 @@ SCRATCH = {
     "hs": ("sbuf", [128, N * 128], "uint8"),
     "yb": ("sbuf", [128, N * 128], "float32"),
 }
-SEMAPHORES = ["ldx", "ldwa", "ldwb", "ldw2", "qx", "qa", "qb", "qw2", "mm0", "mm1", "mm2", "mm3", "sq", "ssarr", "pr",
-              "ss2", "tt", "rtd", "sd", "hd", "hqd", "tA", "tB", "tP", "fA", "fB", "mA", "mB", "mC", "mD1", "mD2",
-              "cpA", "cpB", "cpC", "cpD", "fBl", "lsem", "st"]
+SEMAPHORES = ["ldx", "ldwa", "ldwb", "ldw2", "qx", "q0", "q1", "q2", "q3", "qw2", "mm0", "mm1", "mm2", "mm3", "sqa",
+              "sqb", "ssarr", "pr", "ss2a", "ss2b", "cs", "rtd", "sd", "hd", "hqd", "tA", "tB", "tP", "fA", "fB", "mA",
+              "mB", "mC", "mD1", "mD2", "cpA", "cpB", "cpC", "cpD", "fBl", "lsem", "st"]
 
 
 def _bits(m):
@@ -95,57 +95,63 @@ def rank_program(g, core, T, topo):
         return T.rank_of(at[((q - k) % NCH, dd)])
 
     g.sync.dma_start(T.xb[:], T.x[:, :]).then_inc(S.ldx, 16)
-    g.scalar.dma_start(T.w1b[:, 0:1024], T.w1[:, 0:1024]).then_inc(S.ldwa, 16)
-    g.sync.dma_start(T.w1b[:, 1024:2048], T.w1[:, 1024:2048]).then_inc(S.ldwb, 16)
+    g.scalar.dma_start(T.w1b[:, 0:512], T.w1[:, 0:512]).then_inc(S.ldwa, 16)
+    g.sync.dma_start(T.w1b[:, 512:2048], T.w1[:, 512:2048]).then_inc(S.ldwb, 16)
     g.scalar.dma_start(T.w2b[:], T.w2[:, :]).then_inc(S.ldw2, 16)
 
     v = g.vector
     v.wait_ge(S.ldx, 16)
     v.quantize_mx(T.xq[:], T.xs[:], T.xb[:]).then_inc(S.qx, 1)
     v.wait_ge(S.ldwa, 16)
-    v.quantize_mx(T.w1q[:, 0:256], T.w1s[:, 0:256], T.w1b[:, 0:1024]).then_inc(S.qa, 1)
-    v.wait_ge(S.ldwb, 16)
-    v.quantize_mx(T.w1q[:, 256:512], T.w1s[:, 256:512], T.w1b[:, 1024:2048]).then_inc(S.qb, 1)
+    for i in range(4):
+        if i == 1:
+            v.wait_ge(S.ldwb, 16)
+        v.quantize_mx(T.w1q[:, 128 * i:128 * i + 128], T.w1s[:, 128 * i:128 * i + 128],
+                      T.w1b[:, 512 * i:512 * i + 512]).then_inc(S["q%d" % i], 1)
     v.wait_ge(S.ldw2, 16)
     v.quantize_mx(T.w2q[:], T.w2s[:], T.w2b[:]).then_inc(S.qw2, 1)
 
     te = g.tensor
     te.wait_ge(S.qx, 1)
-    te.wait_ge(S.qa, 1)
     for i in range(4):
-        if i == 2:
-            te.wait_ge(S.qb, 1)
+        te.wait_ge(S["q%d" % i], 1)
         te.matmul_mx(T.z[:, 512 * i:512 * i + 128], T.w1q[:, 128 * i:128 * i + 128], T.w1s[:, 128 * i:128 * i + 128],
                      T.xq[:], T.xs[:], True, True).then_inc(S["mm%d" % i], 1)
     sc = g.scalar
     for i in range(4):
+        col = 0 if i == 0 else 3 + i
         sc.wait_ge(S["mm%d" % i], 1)
         sc.activation(T.junk[:, 128 * i:128 * i + 128], T.z[:, 512 * i:512 * i + 128], A.Square,
-                      accum_out=T.ssl[:, i:i + 1]).then_inc(S.sq, 1)
+                      accum_out=T.own[:, col:col + 1]).then_inc(S.sqa if i == 0 else S.sqb, 1)
 
-    g.wait_ge(S.sq, 4)
+    rid, pid, _ = topo.addr(partner)
+    g.wait_ge(S.sqa, 1)
+    g.remote_dma(T.oth[:, 0:1], T.own[:, 0:1], S.ss2a, S.lsem, pid, rid, off)
+    g.wait_ge(S.sqb, 3)
+    g.remote_dma(T.oth[:, 4:7], T.own[:, 4:7], S.ss2b, S.lsem, pid, rid, off)
+    lcount[0] += 2 * n_off
+    v.wait_ge(S.sqa, 1)
+    v.wait_ge(S.ss2a, n_off)
+    v.tensor_tensor(T.ssl[:, 0:1], T.own[:, 0:1], T.oth[:, 0:1], AluOpType.add).then_inc(S.cs, 1)
+    v.wait_ge(S.sqb, 3)
+    v.wait_ge(S.ss2b, n_off)
+    v.tensor_tensor(T.ssl[:, 1:4], T.own[:, 4:7], T.oth[:, 4:7], AluOpType.add).then_inc(S.cs, 1)
+    g.wait_ge(S.cs, 2)
     g.remote_dma_fused([RemoteDMATransfer(dst_ids=[dst(peer(k)) for k in range(1, NCH)], dma_engine_mask=off,
                                           remote_sem=S.ssarr, srcs=[T.ssl[:, 0:4]],
                                           dsts=[T.ssl[:, 4 * k:4 * k + 4] for k in range(1, NCH)])], local_sem=S.lsem)
     lcount[0] += n_off
     arr = n_off * (NCH - 1)
-    v.wait_ge(S.sq, 4)
+    v.wait_ge(S.cs, 2)
     v.wait_ge(S.ssarr, arr)
     for i in (0, 1):
-        v.tensor_reduce(T.part[:, i:i + 1], T.ssl[:, i:4 * NCH:4], AxisListType.X, AluOpType.add).then_inc(S.pr, 1)
-    sc.wait_ge(S.sq, 4)
+        v.tensor_reduce(T.tot[:, i:i + 1], T.ssl[:, i:4 * NCH:4], AxisListType.X, AluOpType.add).then_inc(S.pr, 1)
+    sc.wait_ge(S.cs, 2)
     sc.wait_ge(S.ssarr, arr)
     for i in (2, 3):
         sc.activation(T.junk2[:, 8 * (i - 2):8 * (i - 2) + NCH], T.ssl[:, i:4 * NCH:4], A.Identity,
-                      accum_out=T.part[:, i:i + 1]).then_inc(S.pr, 1)
-    rid, pid, _ = topo.addr(partner)
-    g.wait_ge(S.pr, 4)
-    g.remote_dma(T.oth[:], T.part[:], S.ss2, S.lsem, pid, rid, off)
-    lcount[0] += n_off
-    v.wait_ge(S.pr, 4)
-    v.wait_ge(S.ss2, n_off)
-    v.tensor_tensor(T.tot[:], T.part[:], T.oth[:], AluOpType.add).then_inc(S.tt, 1)
-    sc.wait_ge(S.tt, 1)
+                      accum_out=T.tot[:, i:i + 1]).then_inc(S.pr, 1)
+    sc.wait_ge(S.pr, 4)
     sc.activation(T.rt[:], T.tot[:], A.Sqrt, bias=EPS, scale=1.0 / (N * NC)).then_inc(S.rtd, 1)
     v.wait_ge(S.rtd, 1)
     v.reciprocal(T.sc[:], T.rt[:]).then_inc(S.sd, 1)

@@ -27,29 +27,22 @@ SCRATCH = {
     "oth": ("sbuf", [128, 8], "float32"),
     "tot": ("sbuf", [128, 4], "float32"),
     "rt": ("sbuf", [128, 4], "float32"),
-    "sc": ("sbuf", [128, 4], "float32"),
+    "vv": ("sbuf", [128, 4], "float32"),
+    "rv": ("sbuf", [128, 4], "float32"),
+    "u": ("sbuf", [128, 512], "float32"),
     "hb": ("sbuf", [128, 512], "bfloat16"),
     "hq": ("sbuf", [128, N * 128], "float8_e4m3fn_x4"),
     "hs": ("sbuf", [128, N * 128], "uint8"),
     "yb": ("sbuf", [128, N * 128], "float32"),
 }
-SEMAPHORES = ["ldx", "ldwa", "ldwb", "ldw2", "qx", "q0", "q1", "q2", "q3", "qw2", "mm0", "mm1", "mm2", "mm3", "sqa",
-              "sqb", "ssarr", "pr", "ss2a", "ss2b", "cs", "rtd", "sd", "hd", "hqd", "tA", "tB", "tP", "fA", "fB", "mA",
-              "mB", "mC", "mD1", "mD2", "cpA", "cpB", "cpC", "cpD", "fBl", "lsem", "st"]
+SEMAPHORES = ["ldx", "ld0", "ld1", "ld2", "ld3", "ldw2", "qx", "q0", "q1", "q2", "q3", "qw2", "mm0", "mm1", "mm2", "mm3",
+              "sqa", "sqb", "ssarr", "pr", "ss2a", "ss2b", "cs", "rtd", "vd", "rvd", "ud", "hd", "hqd", "tAp", "tAc",
+              "tBp", "tBc", "tP", "fA", "fB", "mO", "mP", "mA1", "mA2", "mB", "mC1", "mC2", "mD1", "mD2", "cO", "cP",
+              "cA1", "cA2", "cB", "cC1", "cC2", "cD1", "cD2", "lB", "lsem", "st", "st2"]
 
 
 def _bits(m):
     return bin(m).count("1")
-
-
-def _runs(blocks):
-    out = []
-    for b in sorted(blocks):
-        if out and out[-1][1] == b:
-            out[-1][1] = b + 1
-        else:
-            out.append([b, b + 1])
-    return out
 
 
 def rank_program(g, core, T, topo):
@@ -94,18 +87,21 @@ def rank_program(g, core, T, topo):
         k, dd = (slot, d) if slot < NCH else (slot - NCH, od)
         return T.rank_of(at[((q - k) % NCH, dd)])
 
+    def w1load(queue, i):
+        queue.dma_start(T.w1b[:, 512 * i:512 * i + 512], T.w1[:, 512 * i:512 * i + 512]).then_inc(S["ld%d" % i], 16)
+
     g.sync.dma_start(T.xb[:], T.x[:, :]).then_inc(S.ldx, 16)
-    g.scalar.dma_start(T.w1b[:, 0:512], T.w1[:, 0:512]).then_inc(S.ldwa, 16)
-    g.sync.dma_start(T.w1b[:, 512:2048], T.w1[:, 512:2048]).then_inc(S.ldwb, 16)
-    g.scalar.dma_start(T.w2b[:], T.w2[:, :]).then_inc(S.ldw2, 16)
+    w1load(g.scalar, 0)
+    w1load(g.sync, 1)
+    w1load(g.scalar, 2)
+    w1load(g.sync, 3)
+    g.sync.dma_start(T.w2b[:], T.w2[:, :]).then_inc(S.ldw2, 16)
 
     v = g.vector
     v.wait_ge(S.ldx, 16)
     v.quantize_mx(T.xq[:], T.xs[:], T.xb[:]).then_inc(S.qx, 1)
-    v.wait_ge(S.ldwa, 16)
     for i in range(4):
-        if i == 1:
-            v.wait_ge(S.ldwb, 16)
+        v.wait_ge(S["ld%d" % i], 16)
         v.quantize_mx(T.w1q[:, 128 * i:128 * i + 128], T.w1s[:, 128 * i:128 * i + 128],
                       T.w1b[:, 512 * i:512 * i + 512]).then_inc(S["q%d" % i], 1)
     v.wait_ge(S.ldw2, 16)
@@ -153,94 +149,103 @@ def rank_program(g, core, T, topo):
                       accum_out=T.tot[:, i:i + 1]).then_inc(S.pr, 1)
     sc.wait_ge(S.pr, 4)
     sc.activation(T.rt[:], T.tot[:], A.Sqrt, bias=EPS, scale=1.0 / (N * NC)).then_inc(S.rtd, 1)
-    v.wait_ge(S.rtd, 1)
-    v.reciprocal(T.sc[:], T.rt[:]).then_inc(S.sd, 1)
+    v.wait_ge(S.pr, 4)
+    v.tensor_scalar(T.vv[:], T.tot[:], 1.0 / (N * NC), EPS, AluOpType.mult, AluOpType.add).then_inc(S.vd, 1)
+    v.wait_ge(S.vd, 1)
+    v.reciprocal(T.rv[:], T.vv[:]).then_inc(S.rvd, 1)
+    v.wait_ge(S.rvd, 1)
+    for b in range(4):
+        v.tensor_scalar(T.u[:, 128 * b:128 * b + 128], T.z[:, 512 * b:512 * b + 128], T.rv[:, b:b + 1], None,
+                        AluOpType.mult).then_inc(S.ud, 1)
 
-    v.wait_ge(S.sd, 1)
+    v.wait_ge(S.ud, 4)
+    v.wait_ge(S.rtd, 1)
     for b in (0, 1):
-        v.tensor_scalar(T.hb[:, b:512:4], T.z[:, 512 * b:512 * b + 128], T.sc[:, b:b + 1], None,
+        v.tensor_scalar(T.hb[:, b:512:4], T.u[:, 128 * b:128 * b + 128], T.rt[:, b:b + 1], None,
                         AluOpType.mult).then_inc(S.hd, 1)
-    sc.wait_ge(S.sd, 1)
+    sc.wait_ge(S.ud, 4)
+    sc.wait_ge(S.rtd, 1)
     for b in (2, 3):
-        sc.activation(T.hb[:, b:512:4], T.z[:, 512 * b:512 * b + 128], A.Identity,
-                      scale=T.sc[:, b:b + 1]).then_inc(S.hd, 1)
+        sc.activation(T.hb[:, b:512:4], T.u[:, 128 * b:128 * b + 128], A.Identity,
+                      scale=T.rt[:, b:b + 1]).then_inc(S.hd, 1)
     v.wait_ge(S.hd, 4)
     v.quantize_mx(T.hq[:, 0:128], T.hs[:, 0:128], T.hb[:]).then_inc(S.hqd, 1)
 
     g.wait_ge(S.hqd, 1)
-    for wave, sem in ((WAVE_A, S.tA), (WAVE_B, S.tB)):
+    for wave, semp, semc, lc in ((WAVE_A, S.tAp, S.tAc, S.lsem), (WAVE_B, S.tBp, S.tBc, S.lB)):
         ids = [dst(peer(k)) for k in wave]
-        g.remote_dma_fused([RemoteDMATransfer(dst_ids=ids, dma_engine_mask=off, remote_sem=sem, srcs=[plane(0, 1)],
+        g.remote_dma_fused([RemoteDMATransfer(dst_ids=ids, dma_engine_mask=off, remote_sem=semp, srcs=[plane(0, 1)],
                                               dsts=[plane(k, k + 1) for k in wave])], local_sem=S.lsem)
-        g.remote_dma_fused([RemoteDMATransfer(dst_ids=ids, dma_engine_mask=off, remote_sem=sem, srcs=[codes(0, 1)],
-                                              dsts=[codes(k, k + 1) for k in wave])], local_sem=S.lsem)
-        lcount[0] += 2 * n_off
+        g.remote_dma_fused([RemoteDMATransfer(dst_ids=ids, dma_engine_mask=off, remote_sem=semc, srcs=[codes(0, 1)],
+                                              dsts=[codes(k, k + 1) for k in wave])], local_sem=lc)
+    lcount[0] += 3 * n_off
     g.remote_dma(plane(NCH, NCH + 1), plane(0, 1), S.tP, S.lsem, pid, rid, hi)
     g.remote_dma(codes(NCH, NCH + 1), codes(0, 1), S.tP, S.lsem, pid, rid, hi)
     lcount[0] += 2 * n_hi
-    nA, nB = 2 * n_off * len(WAVE_A), 2 * n_off * len(WAVE_B)
+    nA, nB = n_off * len(WAVE_A), n_off * len(WAVE_B)
     a0, a1 = WAVE_A[0], WAVE_A[-1] + 1
     b0, b1 = WAVE_B[0], WAVE_B[-1] + 1
-    g.wait_ge(S.tA, nA)
+    g.wait_ge(S.tAp, nA)
     g.remote_dma(plane(NCH + a0, NCH + a1), plane(a0, a1), S.fA, S.lsem, pid, rid, hi)
-    g.remote_dma(codes(NCH + a0, NCH + a1), codes(a0, a1), S.fA, S.lsem, pid, rid, hi)
-    lcount[0] += 2 * n_hi
-    g.wait_ge(S.tB, nB)
-    g.remote_dma(plane(NCH + b0, NCH + b1), plane(b0, b1), S.fB, S.fBl, pid, rid, on)
-    g.remote_dma(codes(NCH + b0, NCH + b1), codes(b0, b1), S.fB, S.fBl, pid, rid, on)
+    g.wait_ge(S.tAc, nA)
+    g.remote_dma(codes(NCH + a0, NCH + a1), codes(a0, a1), S.fA, S.lsem, pid, rid, on)
+    g.wait_ge(S.tBp, nB)
+    g.remote_dma(plane(NCH + b0, NCH + b1), plane(b0, b1), S.fB, S.lsem, pid, rid, hi)
+    g.wait_ge(S.tBc, nB)
+    g.remote_dma(codes(NCH + b0, NCH + b1), codes(b0, b1), S.fB, S.lsem, pid, rid, on)
+    lcount[0] += 2 * (n_hi + n_on)
     g.wait_ge(S.lsem, lcount[0])
 
-    def mm(out, a, b, sem):
-        te.matmul_mx(out, T.w2q[:], T.w2s[:], T.hq[:, 128 * a:128 * b], T.hs[:, 128 * a:128 * b],
-                     True, True).then_inc(sem, 1)
+    def bank(i, lo, hi_):
+        buf = T.yp if i < 4 else T.z
+        return buf[:, 512 * (i % 4) + 128 * lo:512 * (i % 4) + 128 * hi_]
 
-    te.wait_ge(S.qw2, 1)
-    te.wait_ge(S.hqd, 1)
-    te.wait_ge(S.tA, nA)
-    mm(T.yp[:, 0:128 * a1], 0, a1, S.mA)
-    te.wait_ge(S.tB, nB)
-    mm(T.yp[:, 512:512 + 128 * (b1 - b0)], b0, b1, S.mB)
-    te.wait_ge(S.tP, 2 * n_hi)
-    te.wait_ge(S.fA, 2 * n_hi)
-    mm(T.yp[:, 1024:1024 + 128 * a1], NCH, NCH + a1, S.mC)
-    te.wait_ge(S.fB, 2 * n_on)
-    mm(T.yp[:, 1536:1536 + 128], NCH + b0, NCH + b0 + 1, S.mD1)
-    mm(T.z[:, 0:128], NCH + b0 + 1, NCH + b1, S.mD2)
+    groups = (("O", 0, 1, 0, True),
+              ("P", NCH, 1, 1, False),
+              ("A1", a0, 2, 2, True),
+              ("A2", a0 + 2, a1 - a0 - 2, 3, False),
+              ("B", b0, b1 - b0, 4, False),
+              ("C1", NCH + a0, 2, 5, True),
+              ("C2", NCH + a0 + 2, a1 - a0 - 2, 6, False),
+              ("D1", NCH + b0, 1, 7, True),
+              ("D2", NCH + b0 + 1, 1, 0, False))
+    needs = {"O": ((S.qw2, 1), (S.hqd, 1)), "P": ((S.tP, 2 * n_hi),), "A1": ((S.tAp, nA), (S.tAc, nA)),
+             "B": ((S.tBp, nB), (S.tBc, nB)), "C1": ((S.fA, n_hi + n_on),), "D1": ((S.fB, n_hi + n_on),),
+             "D2": ((S.cO, 1),)}
 
-    def ycol(slot):
+    def yblk(slot):
         j = block_of(slot)
-        return T.yb[:, 128 * j:128 * j + 128]
+        return slice(128 * j, 128 * j + 128)
 
-    v.wait_ge(S.mA, 1)
-    for t in range(a1):
-        v.tensor_copy(ycol(t), T.yp[:, 128 * t:128 * t + 128]).then_inc(S.cpA, 1)
-    v.wait_ge(S.mC, 1)
-    for t in range(a1):
-        v.tensor_copy(ycol(NCH + t), T.yp[:, 1024 + 128 * t:1024 + 128 * t + 128]).then_inc(S.cpC, 1)
-    v.wait_ge(S.mD1, 1)
-    v.tensor_copy(ycol(NCH + b0), T.yp[:, 1536:1536 + 128]).then_inc(S.cpD, 1)
-    sc.wait_ge(S.mB, 1)
-    for t in range(b1 - b0):
-        sc.activation(ycol(b0 + t), T.yp[:, 512 + 128 * t:512 + 128 * t + 128], A.Copy).then_inc(S.cpB, 1)
-    sc.wait_ge(S.mD2, 1)
-    sc.activation(ycol(NCH + b0 + 1), T.z[:, 0:128], A.Copy).then_inc(S.cpD, 1)
+    nst2 = 0
+    for name, s0, n, bk, on_v in groups:
+        for sem, val in needs.get(name, ()):
+            te.wait_ge(sem, val)
+        te.matmul_mx(bank(bk, 0, n), T.w2q[:], T.w2s[:], T.hq[:, 128 * s0:128 * (s0 + n)],
+                     T.hs[:, 128 * s0:128 * (s0 + n)], True, True).then_inc(S["m" + name], 1)
+        (v if on_v else sc).wait_ge(S["m" + name], 1)
+        for t in range(n):
+            if on_v:
+                v.tensor_copy(T.yb[:, yblk(s0 + t)], bank(bk, t, t + 1)).then_inc(S["c" + name], 1)
+            else:
+                sc.activation(T.yb[:, yblk(s0 + t)], bank(bk, t, t + 1), A.Copy).then_inc(S["c" + name], 1)
+        if name in ("B", "D2"):
+            sc.wait_ge(S["c" + name], n)
+            for t in range(n):
+                sc.dma_start(T.y[:, yblk(s0 + t)], T.yb[:, yblk(s0 + t)]).then_inc(S.st2, 16)
+                nst2 += 16
+    sc.wait_ge(S.st2, nst2)
 
     sy = g.sync
-    nst = 0
+    nst = 16
     sy.wait_ge(S.hqd, 1)
-    sy.wait_ge(S.cpA, a1)
-    sy.wait_ge(S.cpC, a1)
-    sy.wait_ge(S.fBl, 2 * n_on)
-    early = [block_of(t) for t in range(a1)] + [block_of(NCH + t) for t in range(a1)]
-    for lo, hi_ in _runs(early):
-        sy.dma_start(T.y[:, 128 * lo:128 * hi_], T.yb[:, 128 * lo:128 * hi_]).then_inc(S.st, 16)
-        nst += 16
+    sy.wait_ge(S.lB, n_off)
     sy.dma_start(T.h[:, :], T.hb[:]).then_inc(S.st, 16)
-    nst += 16
-    sy.wait_ge(S.cpB, b1 - b0)
-    sy.wait_ge(S.cpD, 2)
-    late = [block_of(t) for t in range(b0, b1)] + [block_of(NCH + t) for t in range(b0, b1)]
-    for lo, hi_ in _runs(late):
-        sy.dma_start(T.y[:, 128 * lo:128 * hi_], T.yb[:, 128 * lo:128 * hi_]).then_inc(S.st, 16)
-        nst += 16
+    for name, s0, n, bk, on_v in groups:
+        if name in ("B", "D2"):
+            continue
+        sy.wait_ge(S["c" + name], n)
+        for t in range(n):
+            sy.dma_start(T.y[:, yblk(s0 + t)], T.yb[:, yblk(s0 + t)]).then_inc(S.st, 16)
+            nst += 16
     sy.wait_ge(S.st, nst)

from concourse.bass import DstId, RemoteDMATransfer
from concourse.mybir import dt, AluOpType, AxisListType, ActivationFunctionType

N = 12
NC = 128
EPS = 0.001
NCH = 6
WAVE_A = (1, 2, 3)
WAVE_B = (4, 5)

SCRATCH = {
    "xb": ("sbuf", [128, 512], "bfloat16"),
    "w1b": ("sbuf", [128, 2048], "bfloat16"),
    "w2b": ("sbuf", [128, 512], "bfloat16"),
    "xq": ("sbuf", [128, 128], "float8_e4m3fn_x4"),
    "xs": ("sbuf", [128, 128], "uint8"),
    "w1q": ("sbuf", [128, 512], "float8_e4m3fn_x4"),
    "w1s": ("sbuf", [128, 512], "uint8"),
    "w2q": ("sbuf", [128, 128], "float8_e4m3fn_x4"),
    "w2s": ("sbuf", [128, 128], "uint8"),
    "z": ("psum", [128, 2048], "float32"),
    "yp": ("psum", [128, 2048], "float32"),
    "junk": ("sbuf", [128, 512], "float32"),
    "junk2": ("sbuf", [128, 16], "float32"),
    "ssl": ("sbuf", [128, 4 * NCH], "float32"),
    "own": ("sbuf", [128, 8], "float32"),
    "oth": ("sbuf", [128, 8], "float32"),
    "tot": ("sbuf", [128, 4], "float32"),
    "rt": ("sbuf", [128, 4], "float32"),
    "vv": ("sbuf", [128, 4], "float32"),
    "rv": ("sbuf", [128, 4], "float32"),
    "u": ("sbuf", [128, 512], "float32"),
    "hb": ("sbuf", [128, 512], "bfloat16"),
    "hq": ("sbuf", [128, N * 128], "float8_e4m3fn_x4"),
    "hs": ("sbuf", [128, N * 128], "uint8"),
    "yb": ("sbuf", [128, N * 128], "float32"),
}
SEMAPHORES = ["ldx", "ld0", "ld1", "ld2", "ld3", "ldw2", "qx", "q0", "q1", "q2", "q3", "qw2", "mm0", "mm1", "mm2", "mm3",
              "sqa", "sqb", "ssarr", "pr", "ss2a", "ss2b", "cs", "rtd", "vd", "rvd", "ud", "hd", "hqd", "tAp", "tAc",
              "tBp", "tBc", "tP", "fA", "fB", "mO", "mP", "mA1", "mA2", "mB", "mC1", "mC2", "mD1", "mD2", "cO", "cP",
              "cA1", "cA2", "cB", "cC1", "cC2", "cD1", "cD2", "lB", "lsem", "st", "st2"]


def _bits(m):
    return bin(m).count("1")


def rank_program(g, core, T, topo):
    rank = T.rank_of(core)
    if rank is None:
        return
    S = T.sem
    A = ActivationFunctionType
    chips = []
    for c in T.cores:
        if topo.chip(c) not in chips:
            chips.append(topo.chip(c))
    at = {}
    for c in T.cores:
        at[(chips.index(topo.chip(c)), topo.die(c))] = c
    q, d = chips.index(topo.chip(core)), topo.die(core)
    partner = [c for c in T.cores if topo.chip(c) == topo.chip(core) and c != core][0]
    od = topo.die(partner)

    def peer(k):
        return at[((q + k) % NCH, d)]

    def dst(c):
        rid, pid, _ = topo.addr(c)
        return DstId(rid=rid, pnc=pid)

    on = topo.mask(core, partner)
    off = on
    for k in range(1, NCH):
        off &= topo.mask(core, peer(k))
    hi = on & ~off
    n_on, n_off, n_hi = _bits(on), _bits(off), _bits(hi)
    lcount = [0]

    def codes(a, b):
        return T.hq[:, 128 * a:128 * b].bitcast(dt.uint8)

    def plane(a, b):
        return T.hs[:, 128 * a:128 * b]

    def block_of(slot):
        k, dd = (slot, d) if slot < NCH else (slot - NCH, od)
        return T.rank_of(at[((q - k) % NCH, dd)])

    def w1load(queue, i):
        queue.dma_start(T.w1b[:, 512 * i:512 * i + 512], T.w1[:, 512 * i:512 * i + 512]).then_inc(S["ld%d" % i], 16)

    g.sync.dma_start(T.xb[:], T.x[:, :]).then_inc(S.ldx, 16)
    w1load(g.scalar, 0)
    w1load(g.sync, 1)
    w1load(g.scalar, 2)
    w1load(g.sync, 3)
    g.sync.dma_start(T.w2b[:], T.w2[:, :]).then_inc(S.ldw2, 16)

    v = g.vector
    v.wait_ge(S.ldx, 16)
    v.quantize_mx(T.xq[:], T.xs[:], T.xb[:]).then_inc(S.qx, 1)
    for i in range(4):
        v.wait_ge(S["ld%d" % i], 16)
        v.quantize_mx(T.w1q[:, 128 * i:128 * i + 128], T.w1s[:, 128 * i:128 * i + 128],
                      T.w1b[:, 512 * i:512 * i + 512]).then_inc(S["q%d" % i], 1)
    v.wait_ge(S.ldw2, 16)
    v.quantize_mx(T.w2q[:], T.w2s[:], T.w2b[:]).then_inc(S.qw2, 1)

    te = g.tensor
    te.wait_ge(S.qx, 1)
    for i in range(4):
        te.wait_ge(S["q%d" % i], 1)
        te.matmul_mx(T.z[:, 512 * i:512 * i + 128], T.w1q[:, 128 * i:128 * i + 128], T.w1s[:, 128 * i:128 * i + 128],
                     T.xq[:], T.xs[:], True, True).then_inc(S["mm%d" % i], 1)
    sc = g.scalar
    for i in range(4):
        col = 0 if i == 0 else 3 + i
        sc.wait_ge(S["mm%d" % i], 1)
        sc.activation(T.junk[:, 128 * i:128 * i + 128], T.z[:, 512 * i:512 * i + 128], A.Square,
                      accum_out=T.own[:, col:col + 1]).then_inc(S.sqa if i == 0 else S.sqb, 1)

    rid, pid, _ = topo.addr(partner)
    g.wait_ge(S.sqa, 1)
    g.remote_dma(T.oth[:, 0:1], T.own[:, 0:1], S.ss2a, S.lsem, pid, rid, off)
    g.wait_ge(S.sqb, 3)
    g.remote_dma(T.oth[:, 4:7], T.own[:, 4:7], S.ss2b, S.lsem, pid, rid, off)
    lcount[0] += 2 * n_off
    v.wait_ge(S.sqa, 1)
    v.wait_ge(S.ss2a, n_off)
    v.tensor_tensor(T.ssl[:, 0:1], T.own[:, 0:1], T.oth[:, 0:1], AluOpType.add).then_inc(S.cs, 1)
    v.wait_ge(S.sqb, 3)
    v.wait_ge(S.ss2b, n_off)
    v.tensor_tensor(T.ssl[:, 1:4], T.own[:, 4:7], T.oth[:, 4:7], AluOpType.add).then_inc(S.cs, 1)
    g.wait_ge(S.cs, 2)
    g.remote_dma_fused([RemoteDMATransfer(dst_ids=[dst(peer(k)) for k in range(1, NCH)], dma_engine_mask=off,
                                          remote_sem=S.ssarr, srcs=[T.ssl[:, 0:4]],
                                          dsts=[T.ssl[:, 4 * k:4 * k + 4] for k in range(1, NCH)])], local_sem=S.lsem)
    lcount[0] += n_off
    arr = n_off * (NCH - 1)
    v.wait_ge(S.cs, 2)
    v.wait_ge(S.ssarr, arr)
    for i in (0, 1):
        v.tensor_reduce(T.tot[:, i:i + 1], T.ssl[:, i:4 * NCH:4], AxisListType.X, AluOpType.add).then_inc(S.pr, 1)
    sc.wait_ge(S.cs, 2)
    sc.wait_ge(S.ssarr, arr)
    for i in (2, 3):
        sc.activation(T.junk2[:, 8 * (i - 2):8 * (i - 2) + NCH], T.ssl[:, i:4 * NCH:4], A.Identity,
                      accum_out=T.tot[:, i:i + 1]).then_inc(S.pr, 1)
    sc.wait_ge(S.pr, 4)
    sc.activation(T.rt[:], T.tot[:], A.Sqrt, bias=EPS, scale=1.0 / (N * NC)).then_inc(S.rtd, 1)
    v.wait_ge(S.pr, 4)
    v.tensor_scalar(T.vv[:], T.tot[:], 1.0 / (N * NC), EPS, AluOpType.mult, AluOpType.add).then_inc(S.vd, 1)
    v.wait_ge(S.vd, 1)
    v.reciprocal(T.rv[:], T.vv[:]).then_inc(S.rvd, 1)
    v.wait_ge(S.rvd, 1)
    for b in range(4):
        v.tensor_scalar(T.u[:, 128 * b:128 * b + 128], T.z[:, 512 * b:512 * b + 128], T.rv[:, b:b + 1], None,
                        AluOpType.mult).then_inc(S.ud, 1)

    v.wait_ge(S.ud, 4)
    v.wait_ge(S.rtd, 1)
    for b in (0, 1):
        v.tensor_scalar(T.hb[:, b:512:4], T.u[:, 128 * b:128 * b + 128], T.rt[:, b:b + 1], None,
                        AluOpType.mult).then_inc(S.hd, 1)
    sc.wait_ge(S.ud, 4)
    sc.wait_ge(S.rtd, 1)
    for b in (2, 3):
        sc.activation(T.hb[:, b:512:4], T.u[:, 128 * b:128 * b + 128], A.Identity,
                      scale=T.rt[:, b:b + 1]).then_inc(S.hd, 1)
    v.wait_ge(S.hd, 4)
    v.quantize_mx(T.hq[:, 0:128], T.hs[:, 0:128], T.hb[:]).then_inc(S.hqd, 1)

    g.wait_ge(S.hqd, 1)
    for wave, semp, semc, lc in ((WAVE_A, S.tAp, S.tAc, S.lsem), (WAVE_B, S.tBp, S.tBc, S.lB)):
        ids = [dst(peer(k)) for k in wave]
        g.remote_dma_fused([RemoteDMATransfer(dst_ids=ids, dma_engine_mask=off, remote_sem=semp, srcs=[plane(0, 1)],
                                              dsts=[plane(k, k + 1) for k in wave])], local_sem=S.lsem)
        g.remote_dma_fused([RemoteDMATransfer(dst_ids=ids, dma_engine_mask=off, remote_sem=semc, srcs=[codes(0, 1)],
                                              dsts=[codes(k, k + 1) for k in wave])], local_sem=lc)
    lcount[0] += 3 * n_off
    g.remote_dma(plane(NCH, NCH + 1), plane(0, 1), S.tP, S.lsem, pid, rid, hi)
    g.remote_dma(codes(NCH, NCH + 1), codes(0, 1), S.tP, S.lsem, pid, rid, hi)
    lcount[0] += 2 * n_hi
    nA, nB = n_off * len(WAVE_A), n_off * len(WAVE_B)
    a0, a1 = WAVE_A[0], WAVE_A[-1] + 1
    b0, b1 = WAVE_B[0], WAVE_B[-1] + 1
    g.wait_ge(S.tAp, nA)
    g.remote_dma(plane(NCH + a0, NCH + a1), plane(a0, a1), S.fA, S.lsem, pid, rid, hi)
    g.wait_ge(S.tAc, nA)
    g.remote_dma(codes(NCH + a0, NCH + a1), codes(a0, a1), S.fA, S.lsem, pid, rid, on)
    g.wait_ge(S.tBp, nB)
    g.remote_dma(plane(NCH + b0, NCH + b1), plane(b0, b1), S.fB, S.lsem, pid, rid, hi)
    g.wait_ge(S.tBc, nB)
    g.remote_dma(codes(NCH + b0, NCH + b1), codes(b0, b1), S.fB, S.lsem, pid, rid, on)
    lcount[0] += 2 * (n_hi + n_on)
    g.wait_ge(S.lsem, lcount[0])

    def bank(i, lo, hi_):
        buf = T.yp if i < 4 else T.z
        return buf[:, 512 * (i % 4) + 128 * lo:512 * (i % 4) + 128 * hi_]

    groups = (("O", 0, 1, 0, True),
              ("P", NCH, 1, 1, False),
              ("A1", a0, 2, 2, True),
              ("A2", a0 + 2, a1 - a0 - 2, 3, False),
              ("B", b0, b1 - b0, 4, False),
              ("C1", NCH + a0, 2, 5, True),
              ("C2", NCH + a0 + 2, a1 - a0 - 2, 6, False),
              ("D1", NCH + b0, 1, 7, True),
              ("D2", NCH + b0 + 1, 1, 0, False))
    needs = {"O": ((S.qw2, 1), (S.hqd, 1)), "P": ((S.tP, 2 * n_hi),), "A1": ((S.tAp, nA), (S.tAc, nA)),
             "B": ((S.tBp, nB), (S.tBc, nB)), "C1": ((S.fA, n_hi + n_on),), "D1": ((S.fB, n_hi + n_on),),
             "D2": ((S.cO, 1),)}

    def yblk(slot):
        j = block_of(slot)
        return slice(128 * j, 128 * j + 128)

    nst2 = 0
    for name, s0, n, bk, on_v in groups:
        for sem, val in needs.get(name, ()):
            te.wait_ge(sem, val)
        te.matmul_mx(bank(bk, 0, n), T.w2q[:], T.w2s[:], T.hq[:, 128 * s0:128 * (s0 + n)],
                     T.hs[:, 128 * s0:128 * (s0 + n)], True, True).then_inc(S["m" + name], 1)
        (v if on_v else sc).wait_ge(S["m" + name], 1)
        for t in range(n):
            if on_v:
                v.tensor_copy(T.yb[:, yblk(s0 + t)], bank(bk, t, t + 1)).then_inc(S["c" + name], 1)
            else:
                sc.activation(T.yb[:, yblk(s0 + t)], bank(bk, t, t + 1), A.Copy).then_inc(S["c" + name], 1)
        if name in ("B", "D2"):
            sc.wait_ge(S["c" + name], n)
            for t in range(n):
                sc.dma_start(T.y[:, yblk(s0 + t)], T.yb[:, yblk(s0 + t)]).then_inc(S.st2, 16)
                nst2 += 16
    sc.wait_ge(S.st2, nst2)

    sy = g.sync
    nst = 16
    sy.wait_ge(S.hqd, 1)
    sy.wait_ge(S.lB, n_off)
    sy.dma_start(T.h[:, :], T.hb[:]).then_inc(S.st, 16)
    for name, s0, n, bk, on_v in groups:
        if name in ("B", "D2"):
            continue
        sy.wait_ge(S["c" + name], n)
        for t in range(n):
            sy.dma_start(T.y[:, yblk(s0 + t)], T.yb[:, yblk(s0 + t)]).then_inc(S.st, 16)
            nst += 16
    sy.wait_ge(S.st, nst)
